import numpy as np
import ml_dtypes


def mxq(x, axis, fmt="e4m3"):
    dtype, down = {"e4m3": (ml_dtypes.float8_e4m3fn, 7), "e5m2": (ml_dtypes.float8_e5m2, 14)}[fmt]
    v = np.moveaxis(np.asarray(x, np.float32).astype(ml_dtypes.bfloat16).astype(np.float64), axis, -1)
    blocks = v.reshape(v.shape[:-1] + (-1, 32))
    amax = np.abs(blocks).max(-1, keepdims=True)
    byte = np.maximum(np.where(amax > 0, np.frexp(amax)[1] - 1 + 127, 0) - down, 1)
    scale = np.exp2(byte - 127.0)
    codes = (blocks / scale).astype(np.float32).astype(dtype).astype(np.float64)
    return np.moveaxis((codes * scale).reshape(v.shape), -1, axis)


WIDE = False


def mx_kscale(k):
    if not WIDE:
        return np.ones(k)
    levels = np.array([10, -10, 5, -5, 0])
    if k % 512:
        return np.exp2(np.random.permutation(np.resize(levels, k // 32))).repeat(32)
    a = np.empty((k // 512, 16))
    for p in range(k // 512):
        a[p, :8] = np.random.permutation(np.resize(levels, 8))
        for g in range(8):
            far = levels[np.abs(levels - a[p, g]) >= 10]
            a[p, g + 8] = far[np.random.randint(len(far))]
    return np.exp2(a.ravel()).repeat(32)


def f64(x):
    return np.asarray(x).astype(np.float64)


def striped(idx):
    return np.tile(idx.reshape(-1, 16).T, (8, 1)).astype(np.uint16)


def unstriped(offs):
    return offs[:16].T.reshape(-1).astype(np.int64)


E2M1 = np.array([0.0, 0.5, 1.0, 1.5, 2.0, 3.0, 4.0, 6.0, -0.0, -0.5, -1.0, -1.5, -2.0, -3.0, -4.0, -6.0])


def pack_weight(w, fmt):
    k, n = w.shape
    w = f64(np.asarray(w, np.float32).astype(ml_dtypes.bfloat16)).reshape(k // 32, 32, n)
    amax = np.abs(w).max(1)
    if fmt == "e4m3":
        byte = np.frexp(amax)[1] - 1 + 127 - 7
    else:
        mant, ex = np.frexp(amax / 6.0)
        byte = np.where(mant > 0.5, ex, ex - 1) + 127
    byte = np.clip(np.where(amax > 0, byte, 1), 1, 254)
    scaled = (w * np.exp2(127.0 - byte)[:, None, :]).reshape(k, n).astype(np.float32)
    by_word = np.ascontiguousarray(scaled.reshape(k // 512, 128, 4, n).transpose(0, 1, 3, 2))
    if fmt == "e4m3":
        words = by_word.astype(ml_dtypes.float8_e4m3fn).view(np.uint8)
    else:
        c = by_word.astype(ml_dtypes.float4_e2m1fn).view(np.uint8) & 0xF
        words = (c[..., 0::2] | (c[..., 1::2] << 4)).reshape(k // 512, 128, 2 * n)
    return np.ascontiguousarray(words), np.ascontiguousarray(byte.astype(np.uint8).reshape(k // 512, 16, n))


def unpack_weight(words, scales, fmt):
    g, _, n = scales.shape
    words = np.ascontiguousarray(words).reshape(g, 128, n, -1)
    if fmt == "e4m3":
        vals = words.view(ml_dtypes.float8_e4m3fn).astype(np.float64)
    else:
        nib = np.empty((g, 128, n, 4), np.uint8)
        nib[..., 0::2] = words & 0xF
        nib[..., 1::2] = words >> 4
        vals = E2M1[nib]
    vals = vals * np.repeat(np.exp2(scales.astype(np.float64) - 127.0), 8, axis=1)[..., None]
    return vals.transpose(0, 1, 3, 2).reshape(g * 512, n)


def gelu(v):
    return 0.5 * v * (1.0 + np.tanh(np.sqrt(2.0 / np.pi) * (v + 0.044715 * v**3)))


T, S, T3, P, K, K2, H, N = 4096, 1024, 2048, 512, 1536, 1024, 512, 768

def setup_inputs():
    n = np.random.standard_normal
    s = mx_kscale(K)[:, None]
    s2 = mx_kscale(K2)[:, None]
    u = mx_kscale(H)[:, None]
    d = {}
    d["tab_words"], d["tab_scales"] = pack_weight(n((K, T)) * s, "e4m3")
    d["offs"] = striped(np.random.permutation(T)[:S])
    d["tab2_words"], d["tab2_scales"] = pack_weight(n((K2, T3)) * s2, "e4m3")
    d["offs2"] = striped(np.random.permutation(T3)[:P])
    d["pos1"] = striped(np.random.permutation(S)[:P])
    d["w1"] = (n((K, H)) / K ** 0.5 / s * u.T).astype(np.float32)
    d["w2"] = (1.3 * n((K2, H)) / K2 ** 0.5 / s2).astype(np.float32)
    d["duty"] = np.exp(0.5 * n((H, S))).astype(np.float32)
    d["wgs"] = np.exp(0.3 * n((128, P))).astype(np.float32)
    d["w4_words"], d["w4_scales"] = pack_weight(1.8 * n((H, N)) / H ** 0.5 / u, "e2m1")
    d["w5"] = (n((H, N)) / H ** 0.5 / u).astype(np.float32)
    return d

def reference(tab_words, tab_scales, offs, tab2_words, tab2_scales, offs2, pos1, w1, w2, duty, wgs, w4_words, w4_scales, w5):
    v = unpack_weight(tab_words, tab_scales, "e4m3")[:, unstriped(offs)]
    v2 = unpack_weight(tab2_words, tab2_scales, "e4m3")[:, unstriped(offs2)]
    a = (mxq(f64(w1), 0, "e4m3").T @ v) * f64(duty)
    b = np.square(mxq(f64(w2), 0, "e4m3").T @ v2)
    placed = np.zeros((H, S))
    placed[:, unstriped(pos1)] = np.tile(f64(wgs), (H // 128, 1)) * b
    z = a / (1.0 + placed)
    w4 = unpack_weight(w4_words, w4_scales, "e2m1")
    yz = w4.T @ mxq(z, 0, "e4m3")
    ya = mxq(f64(w5), 0, "e4m3").T @ mxq(a, 0, "e4m3")
    return np.maximum(yz, ya)

@@ -1,0 +1,287 @@
+from contextlib import ExitStack
+
+import concourse.mybir as mybir
+from concourse.masks import make_identity
+
+T, S, T3, L, K, K2, H, N = 4096, 1024, 2048, 512, 1536, 1024, 512, 768
+FLOPS = 2 * (K * H * S + K2 * H * L + 2 * H * N * S)
+
+F32 = mybir.dt.float32
+BF16 = mybir.dt.bfloat16
+I32 = mybir.dt.int32
+U32 = mybir.dt.uint32
+U16 = mybir.dt.uint16
+U8 = mybir.dt.uint8
+FP8X4 = mybir.dt.float8_e4m3fn_x4
+FP4X4 = mybir.dt.float4_e2m1fn_x4
+MULT = mybir.AluOpType.mult
+MAX = mybir.AluOpType.max
+ACT = mybir.ActivationFunctionType
+
+P = 128
+PACK = 4
+K_PASS = P * PACK
+BANK = 512
+QUADS = 4
+HALVES = S // BANK
+
+
+def tile_list_chain_wear_features_kernel(
+    tc, tab_words, tab_scales, offs, tab2_words, tab2_scales, offs2, pos1, w1, w2, duty, wgs, w4_words, w4_scales, w5, out
+):
+    nc = tc.nc
+    passes1 = K // K_PASS
+    passes2 = K2 // K_PASS
+
+    with ExitStack() as ctx:
+        keep = ctx.enter_context(tc.tile_pool(name="keep", bufs=1))
+        ring = ctx.enter_context(tc.tile_pool(name="ring", bufs=1))
+        psum = ctx.enter_context(tc.psum_pool(name="psum", bufs=1))
+
+        def bank(i):
+            return psum.tile([P, BANK], F32, name=f"bank{i}")
+
+        def load_list(src, name):
+            tile = keep.tile(list(src.shape), U16, name=name)
+            nc.sync.dma_start(tile[:], src)
+            return tile
+
+        def load_scale_rows(src, name, queue):
+            passes, rows, width = src.shape
+            tile = keep.tile([P, width], U8, name=name, align_bytes=64)
+            nc.vector.memset(tile[:].bitcast(I32), 0)
+            for q in range(QUADS):
+                queue.dma_start(
+                    out=tile[32 * q : 32 * q + 4 * passes, :].bitcast(I32),
+                    in_=src[:, 4 * q : 4 * q + 4, :].bitcast(I32),
+                )
+            return tile
+
+        def load_words(src, name):
+            tile = ring.tile([P, src.shape[1]], U32, name=name, bufs=3, align_bytes=64)
+            nc.sync.dma_start(out=tile[:].bitcast(I32), in_=src.rearrange("p t i -> p (t i)").bitcast(I32))
+            return tile
+
+        def load_rows(src, name):
+            tile = ring.tile([P, PACK, src.shape[1]], F32, name=name)
+            nc.sync.dma_start(out=tile[:], in_=src.rearrange("(p j) w -> p j w", j=PACK))
+            return tile
+
+        def gather(window, offsets, count, dtype, name):
+            tile = keep.tile([P, count], dtype, name=name, align_bytes=64)
+            nc.vector.tensor_copy(tile[:], window[:].indirect(offsets))
+            return tile
+
+        def staged(width):
+            return ring.tile([P, PACK * width], BF16, name="staged", bufs=4, align_bytes=64)
+
+        def round_dealt(raw):
+            tile = staged(H)
+            nc.scalar.copy(
+                out=tile[:].rearrange("p (t m j) -> p m j t", t=PACK, j=PACK),
+                in_=raw[:].rearrange("p j (m t) -> p m j t", t=PACK),
+            )
+            return tile
+
+        def woven(tile):
+            return tile[:].rearrange("p (c i j) -> p c j i", i=4, j=PACK)
+
+        def by_fours(rows):
+            return rows.rearrange("p j (c i) -> p c j i", i=4)
+
+        def quantise(rounded, name):
+            width = rounded.shape[1] // PACK
+            codes = keep.tile([P, width], U32, name=name + "_codes", align_bytes=64)
+            scales = keep.tile([P, width], U8, name=name + "_scales", align_bytes=64)
+            nc.vector.quantize_mx(out=codes[:].bitcast(FP8X4), scales=scales[:], in_=rounded[:])
+            return codes, scales
+
+        def first_stage_pass(acc, weight, t, words, scale_rows, a, passes):
+            cols = slice(t * P, (t + 1) * P)
+            nc.tensor.matmul_mx(
+                out=acc[:],
+                lhsT=weight[0][:, cols].bitcast(FP8X4),
+                lhsT_scale=weight[1][:, cols],
+                rhs=words.bitcast(FP8X4),
+                rhs_scale=scale_rows,
+                start=(a == 0),
+                stop=(a == passes - 1),
+            )
+
+        ident = keep.tile([P, P], F32, name="ident")
+        make_identity(nc, ident[:])
+        s1 = load_scale_rows(tab_scales, "s1", nc.gpsimd)
+        s2 = load_scale_rows(tab2_scales, "s2", nc.gpsimd)
+        wg = ring.tile([P, L], F32, name="result", bufs=4)
+        nc.sync.dma_start(out=wg[:], in_=wgs)
+        raw2 = [load_rows(w2[0:K_PASS, :], "raw0")]
+        list2 = load_list(offs2, "list2")
+        list1 = load_list(offs, "list1")
+        places = load_list(pos1, "places")
+        words2 = [load_words(tab2_words[0], "quad")]
+        raw2.append(load_rows(w2[K_PASS : 2 * K_PASS, :], "raw1"))
+        words2.append(load_words(tab2_words[1], "quad"))
+
+        pages = []
+        for t in range(PACK):
+            page = keep.tile([P, S], F32, name=f"page{t}")
+            nc.vector.memset(page[:], 0.0)
+            pages.append(page)
+
+        turned = bank(7)
+        for b in range(L // P):
+            nc.tensor.transpose(turned[:, b * P : (b + 1) * P], wg[:, b * P : (b + 1) * P], ident[:])
+        spread = ring.tile([P, L // P, PACK, QUADS, 32], F32, name="quad", bufs=3, align_bytes=64)
+        for q in range(QUADS):
+            nc.scalar.copy(out=spread[:, :, :, q, :], in_=turned[:].rearrange("p (b m t) -> p b t m", b=L // P, t=PACK))
+
+        gs1 = gather(s1, list1[:], S, U8, "gs1")
+        gs2 = gather(s2, list2[:], L, U8, "gs2")
+
+        rounded2 = [round_dealt(raw2[0])]
+        g2 = [gather(words2[0], list2[:], L, U32, "g2_0")]
+        w2q = [quantise(rounded2[0], "w2_0")]
+
+        dealt, backs = [], []
+        for t in range(PACK):
+            back = bank(t)
+            for b in range(L // P):
+                nc.tensor.transpose(
+                    back[:, b * P : (b + 1) * P], spread[:, b, t, :, :].rearrange("p q m -> p (q m)"), ident[:]
+                )
+            backs.append(back)
+
+        def deal(t):
+            tile = keep.tile([P, L], F32, name=f"dealt{t}")
+            nc.scalar.copy(out=tile[:], in_=backs[t][:])
+            dealt.append(tile)
+
+        deal(0)
+        deal(1)
+
+        rounded2.append(round_dealt(raw2[1]))
+        w2q.append(quantise(rounded2[1], "w2_1"))
+        g2.append(gather(words2[1], list2[:], L, U32, "s1"))
+
+        acc2 = [bank(4 + t) for t in range(PACK)]
+        for a in range(passes2):
+            for t in range(PACK):
+                first_stage_pass(acc2[t], w2q[a], t, g2[a][:], gs2[4 * a : P, :], a, passes2)
+
+        words1, raw1 = [], []
+        for a in range(passes1):
+            if a < passes1 - 1:
+                words1.append(load_words(tab_words[a], "words"))
+                raw1.append(load_rows(w1[a * K_PASS : (a + 1) * K_PASS, :], f"raw{2 + a}"))
+            else:
+                raw1.append(load_rows(w1[a * K_PASS : (a + 1) * K_PASS, :], f"raw{2 + a}"))
+                words1.append(load_words(tab_words[a], "words"))
+        duty_rows = [load_rows(duty[:, 0:BANK], "raw0")]
+        s4 = load_scale_rows(w4_scales, "s4", nc.sync)
+        w4 = keep.tile([P, 2 * N], U8, name="w4", align_bytes=64)
+        nc.sync.dma_start(out=w4[:].bitcast(I32), in_=w4_words[0].bitcast(I32))
+        raw5 = [load_rows(w5[:, 0:BANK], "raw1")]
+
+        damp = keep.tile([P, PACK, S], F32, name="damp")
+        squares = []
+        for t in range(PACK):
+            sq = ring.tile([P, L], F32, name="evac", bufs=4)
+            nc.scalar.activation(out=sq[:], in_=acc2[t][:], func=ACT.Square)
+            squares.append(sq)
+        deal(2)
+        deal(3)
+        for t in range(PACK):
+            nc.vector.tensor_tensor(pages[t][:].indirect(places[:]), squares[t][:], dealt[t][:], MULT)
+
+        def damping(t, name):
+            logs = ring.tile([P, S], F32, name=name)
+            nc.scalar.activation(out=logs[:], in_=pages[t][:], func=ACT.Abs_reciprocal_sqrt, bias=1.0)
+            nc.scalar.activation(out=damp[:, t, :], in_=logs[:], func=ACT.Square)
+
+        acc1 = [[bank(PACK * h + t) for t in range(PACK)] for h in range(HALVES)]
+
+        def first_stage(a, rounded):
+            if a < passes1 - 1:
+                whole = gather(words1[a], list1[:], S, U32, f"g1_{a}")
+                picked = [whole[:, h * BANK : (h + 1) * BANK] for h in range(HALVES)]
+                wq = quantise(rounded, f"w1_{a}")
+            else:
+                wq = quantise(rounded, f"w1_{a}")
+                picked = [
+                    gather(words1[a], list1[:, h * BANK // 16 : (h + 1) * BANK // 16], BANK, U32, f"g1_{a}_{h}")[:]
+                    for h in range(HALVES)
+                ]
+            for h in range(HALVES):
+                for t in range(PACK):
+                    first_stage_pass(acc1[h][t], wq, t, picked[h], gs1[4 * a : P, h * BANK : (h + 1) * BANK], a, passes1)
+
+        nc.scalar.activation(out=damp[:, 0, :], in_=pages[0][:], func=ACT.Abs_reciprocal_sqrt, bias=1.0)
+        nc.scalar.activation(out=damp[:, 0, :], in_=damp[:, 0, :], func=ACT.Square)
+        first_stage(0, round_dealt(raw1[0]))
+        damping(1, "raw2")
+        damping(2, "raw2")
+        raw5.append(load_rows(w5[:, BANK:N], "raw2"))
+        first_stage(1, round_dealt(raw1[1]))
+        duty_rows.append(load_rows(duty[:, BANK:S], "raw3"))
+        first_stage(2, round_dealt(raw1[2]))
+        damping(3, "raw4")
+
+        w5q = []
+        for part, raw in enumerate(raw5):
+            rounded = staged(raw.shape[2])
+            nc.scalar.copy(out=woven(rounded), in_=by_fours(raw[:]))
+            w5q.append(rounded)
+
+        def weigh(h):
+            a32 = ring.tile([P, PACK, BANK], F32, name="quad", bufs=3, align_bytes=64)
+            for t in range(PACK):
+                nc.vector.tensor_tensor(a32[:, t, :], acc1[h][t][:], duty_rows[h][:, t, :], MULT)
+            return a32
+
+        def round_a(a32):
+            tile = staged(BANK)
+            nc.scalar.copy(out=woven(tile), in_=by_fours(a32[:]))
+            return tile
+
+        def round_z(a32, h):
+            tile = staged(BANK)
+            nc.vector.tensor_tensor(woven(tile), by_fours(a32[:]), by_fours(damp[:, :, h * BANK : (h + 1) * BANK]), MULT)
+            return tile
+
+        def second_stage(h, n, aq, zq):
+            pair = (h * (N // P) + n) % PACK
+            part, first = divmod(n * P, BANK)
+            cols = slice(first, first + P)
+            ya, yz = bank(2 * pair), bank(2 * pair + 1)
+            nc.tensor.matmul_mx(
+                out=ya[:], lhsT=w5q[part][0][:, cols].bitcast(FP8X4), lhsT_scale=w5q[part][1][:, cols],
+                rhs=aq[0][:].bitcast(FP8X4), rhs_scale=aq[1][:], start=True, stop=True,
+            )
+            nc.tensor.matmul_mx(
+                out=yz[:], lhsT=w4[:, 2 * n * P : 2 * (n + 1) * P].bitcast(FP4X4), lhsT_scale=s4[:, n * P : (n + 1) * P],
+                rhs=zq[0][:].bitcast(FP8X4), rhs_scale=zq[1][:], start=True, stop=True,
+            )
+            ya_sb = ring.tile([P, BANK], F32, name="evac", bufs=4)
+            nc.scalar.copy(out=ya_sb[:], in_=ya[:])
+            result = ring.tile([P, BANK], F32, name="result", bufs=4)
+            nc.vector.tensor_tensor(result[:], yz[:], ya_sb[:], MAX)
+            nc.sync.dma_start(out=out[n * P : (n + 1) * P, h * BANK : (h + 1) * BANK], in_=result[:])
+
+        a0 = weigh(0)
+        w5q[0] = quantise(w5q[0], "w5_0")
+        w5q[1] = quantise(w5q[1], "w5_1")
+        ra0 = round_a(a0)
+        rz0 = round_z(a0, 0)
+        a1 = weigh(1)
+        ra1 = round_a(a1)
+        zq0 = quantise(rz0, "z0")
+        aq0 = quantise(ra0, "a0")
+        rz1 = round_z(a1, 1)
+        for n in range(3):
+            second_stage(0, n, aq0, zq0)
+        zq1 = quantise(rz1, "z1")
+        aq1 = quantise(ra1, "a1")
+        for n in range(3, N // P):
+            second_stage(0, n, aq0, zq0)
+        for n in range(N // P):
+            second_stage(1, n, aq1, zq1)

@@ -34,21 +34,23 @@ def tile_list_chain_wear_features_kernel(
     passes2 = K2 // K_PASS
 
     with ExitStack() as ctx:
-        keep = ctx.enter_context(tc.tile_pool(name="keep", bufs=1))
-        ring = ctx.enter_context(tc.tile_pool(name="ring", bufs=1))
+        sbuf = ctx.enter_context(tc.tile_pool(name="sbuf", bufs=1))
         psum = ctx.enter_context(tc.psum_pool(name="psum", bufs=1))
+
+        def place(shape, dtype, room, bufs=1):
+            return sbuf.tile(shape, dtype, name=room, bufs=bufs, align_bytes=64)
 
         def bank(i):
             return psum.tile([P, BANK], F32, name=f"bank{i}")
 
-        def load_list(src, name):
-            tile = keep.tile(list(src.shape), U16, name=name)
+        def load_list(src, room):
+            tile = place(list(src.shape), U16, room)
             nc.sync.dma_start(tile[:], src)
             return tile
 
-        def load_scale_rows(src, name, queue):
+        def load_scale_rows(src, room, queue):
             passes, rows, width = src.shape
-            tile = keep.tile([P, width], U8, name=name, align_bytes=64)
+            tile = place([P, width], U8, room)
             nc.vector.memset(tile[:].bitcast(I32), 0)
             for q in range(QUADS):
                 queue.dma_start(
@@ -57,26 +59,23 @@ def tile_list_chain_wear_features_kernel(
                 )
             return tile
 
-        def load_words(src, name):
-            tile = ring.tile([P, src.shape[1]], U32, name=name, bufs=3, align_bytes=64)
+        def load_words(src, room):
+            tile = place([P, src.shape[1]], U32, room)
             nc.sync.dma_start(out=tile[:].bitcast(I32), in_=src.rearrange("p t i -> p (t i)").bitcast(I32))
             return tile
 
-        def load_rows(src, name):
-            tile = ring.tile([P, PACK, src.shape[1]], F32, name=name)
+        def load_rows(src, room):
+            tile = place([P, PACK, src.shape[1]], F32, room)
             nc.sync.dma_start(out=tile[:], in_=src.rearrange("(p j) w -> p j w", j=PACK))
             return tile
 
-        def gather(window, offsets, count, dtype, name):
-            tile = keep.tile([P, count], dtype, name=name, align_bytes=64)
+        def gather(window, offsets, count, dtype, room):
+            tile = place([P, count], dtype, room)
             nc.vector.tensor_copy(tile[:], window[:].indirect(offsets))
             return tile
 
-        def staged(width):
-            return ring.tile([P, PACK * width], BF16, name="staged", bufs=4, align_bytes=64)
-
-        def round_dealt(raw):
-            tile = staged(H)
+        def round_dealt(raw, room):
+            tile = place([P, PACK * H], BF16, room)
             nc.scalar.copy(
                 out=tile[:].rearrange("p (t m j) -> p m j t", t=PACK, j=PACK),
                 in_=raw[:].rearrange("p j (m t) -> p m j t", t=PACK),
@@ -89,10 +88,15 @@ def tile_list_chain_wear_features_kernel(
         def by_fours(rows):
             return rows.rearrange("p j (c i) -> p c j i", i=4)
 
+        def round_plain(rows, room):
+            tile = place([P, PACK * rows.shape[2]], BF16, room)
+            nc.scalar.copy(out=woven(tile), in_=by_fours(rows[:]))
+            return tile
+
         def quantise(rounded, name):
             width = rounded.shape[1] // PACK
-            codes = keep.tile([P, width], U32, name=name + "_codes", align_bytes=64)
-            scales = keep.tile([P, width], U8, name=name + "_scales", align_bytes=64)
+            codes = place([P, width], U32, name + "_codes")
+            scales = place([P, width], U8, name + "_scales")
             nc.vector.quantize_mx(out=codes[:].bitcast(FP8X4), scales=scales[:], in_=rounded[:])
             return codes, scales
 
@@ -108,39 +112,33 @@ def tile_list_chain_wear_features_kernel(
                 stop=(a == passes - 1),
             )
 
-        ident = keep.tile([P, P], F32, name="ident")
+        ident = place([P, P], F32, "ident")
         make_identity(nc, ident[:])
         s1 = load_scale_rows(tab_scales, "s1", nc.gpsimd)
         s2 = load_scale_rows(tab2_scales, "s2", nc.gpsimd)
-        wg = ring.tile([P, L], F32, name="result", bufs=4)
+        wg = place([P, L], F32, "wg")
         nc.sync.dma_start(out=wg[:], in_=wgs)
         raw2 = [load_rows(w2[0:K_PASS, :], "raw0")]
         list2 = load_list(offs2, "list2")
         list1 = load_list(offs, "list1")
         places = load_list(pos1, "places")
-        words2 = [load_words(tab2_words[0], "quad")]
+        words2 = [load_words(tab2_words[0], "words2_0")]
         raw2.append(load_rows(w2[K_PASS : 2 * K_PASS, :], "raw1"))
-        words2.append(load_words(tab2_words[1], "quad"))
-
-        pages = []
-        for t in range(PACK):
-            page = keep.tile([P, S], F32, name=f"page{t}")
-            nc.vector.memset(page[:], 0.0)
-            pages.append(page)
+        words2.append(load_words(tab2_words[1], "words2_1"))
 
         turned = bank(7)
         for b in range(L // P):
             nc.tensor.transpose(turned[:, b * P : (b + 1) * P], wg[:, b * P : (b + 1) * P], ident[:])
-        spread = ring.tile([P, L // P, PACK, QUADS, 32], F32, name="quad", bufs=3, align_bytes=64)
+        spread = place([P, L // P, PACK, QUADS, 32], F32, "spread")
         for q in range(QUADS):
             nc.scalar.copy(out=spread[:, :, :, q, :], in_=turned[:].rearrange("p (b m t) -> p b t m", b=L // P, t=PACK))
 
         gs1 = gather(s1, list1[:], S, U8, "gs1")
         gs2 = gather(s2, list2[:], L, U8, "gs2")
 
-        rounded2 = [round_dealt(raw2[0])]
+        rounded = round_dealt(raw2[0], "rounded0")
         g2 = [gather(words2[0], list2[:], L, U32, "g2_0")]
-        w2q = [quantise(rounded2[0], "w2_0")]
+        w2q = [quantise(rounded, "w2_0")]
 
         dealt, backs = [], []
         for t in range(PACK):
@@ -152,16 +150,21 @@ def tile_list_chain_wear_features_kernel(
             backs.append(back)
 
         def deal(t):
-            tile = keep.tile([P, L], F32, name=f"dealt{t}")
+            tile = place([P, L], F32, f"dealt{t}")
             nc.scalar.copy(out=tile[:], in_=backs[t][:])
             dealt.append(tile)
 
         deal(0)
         deal(1)
 
-        rounded2.append(round_dealt(raw2[1]))
-        w2q.append(quantise(rounded2[1], "w2_1"))
+        w2q.append(quantise(round_dealt(raw2[1], "rounded1"), "w2_1"))
         g2.append(gather(words2[1], list2[:], L, U32, "s1"))
+
+        pages = []
+        for room in ("wg", "spread", "words2_0", "s2"):
+            page = place([P, S], F32, room)
+            nc.gpsimd.memset(page[:], 0.0)
+            pages.append(page)
 
         acc2 = [bank(4 + t) for t in range(PACK)]
         for a in range(passes2):
@@ -171,21 +174,21 @@ def tile_list_chain_wear_features_kernel(
         words1, raw1 = [], []
         for a in range(passes1):
             if a < passes1 - 1:
-                words1.append(load_words(tab_words[a], "words"))
+                words1.append(load_words(tab_words[a], f"words1_{a}"))
                 raw1.append(load_rows(w1[a * K_PASS : (a + 1) * K_PASS, :], f"raw{2 + a}"))
             else:
                 raw1.append(load_rows(w1[a * K_PASS : (a + 1) * K_PASS, :], f"raw{2 + a}"))
-                words1.append(load_words(tab_words[a], "words"))
+                words1.append(load_words(tab_words[a], f"words1_{a}"))
         duty_rows = [load_rows(duty[:, 0:BANK], "raw0")]
         s4 = load_scale_rows(w4_scales, "s4", nc.sync)
-        w4 = keep.tile([P, 2 * N], U8, name="w4", align_bytes=64)
+        w4 = place([P, 2 * N], U8, "w4")
         nc.sync.dma_start(out=w4[:].bitcast(I32), in_=w4_words[0].bitcast(I32))
         raw5 = [load_rows(w5[:, 0:BANK], "raw1")]
 
-        damp = keep.tile([P, PACK, S], F32, name="damp")
+        damp = place([P, PACK, S], F32, "damp")
         squares = []
         for t in range(PACK):
-            sq = ring.tile([P, L], F32, name="evac", bufs=4)
+            sq = place([P, L], F32, f"square{t}")
             nc.scalar.activation(out=sq[:], in_=acc2[t][:], func=ACT.Square)
             squares.append(sq)
         deal(2)
@@ -193,58 +196,49 @@ def tile_list_chain_wear_features_kernel(
         for t in range(PACK):
             nc.vector.tensor_tensor(pages[t][:].indirect(places[:]), squares[t][:], dealt[t][:], MULT)
 
-        def damping(t, name):
-            logs = ring.tile([P, S], F32, name=name)
-            nc.scalar.activation(out=logs[:], in_=pages[t][:], func=ACT.Abs_reciprocal_sqrt, bias=1.0)
-            nc.scalar.activation(out=damp[:, t, :], in_=logs[:], func=ACT.Square)
+        def damping(t, room):
+            root = place([P, S], F32, room)
+            nc.scalar.activation(out=root[:], in_=pages[t][:], func=ACT.Abs_reciprocal_sqrt, bias=1.0)
+            nc.scalar.activation(out=damp[:, t, :], in_=root[:], func=ACT.Square)
 
         acc1 = [[bank(PACK * h + t) for t in range(PACK)] for h in range(HALVES)]
 
-        def first_stage(a, rounded):
-            if a < passes1 - 1:
-                whole = gather(words1[a], list1[:], S, U32, f"g1_{a}")
+        def first_stage(a, rooms):
+            rounded = round_dealt(raw1[a], f"dealt{a}")
+            if len(rooms) == 1:
+                whole = gather(words1[a], list1[:], S, U32, rooms[0])
                 picked = [whole[:, h * BANK : (h + 1) * BANK] for h in range(HALVES)]
                 wq = quantise(rounded, f"w1_{a}")
             else:
                 wq = quantise(rounded, f"w1_{a}")
                 picked = [
-                    gather(words1[a], list1[:, h * BANK // 16 : (h + 1) * BANK // 16], BANK, U32, f"g1_{a}_{h}")[:]
+                    gather(words1[a], list1[:, h * BANK // 16 : (h + 1) * BANK // 16], BANK, U32, rooms[h])[:]
                     for h in range(HALVES)
                 ]
             for h in range(HALVES):
                 for t in range(PACK):
                     first_stage_pass(acc1[h][t], wq, t, picked[h], gs1[4 * a : P, h * BANK : (h + 1) * BANK], a, passes1)
 
-        nc.scalar.activation(out=damp[:, 0, :], in_=pages[0][:], func=ACT.Abs_reciprocal_sqrt, bias=1.0)
-        nc.scalar.activation(out=damp[:, 0, :], in_=damp[:, 0, :], func=ACT.Square)
-        first_stage(0, round_dealt(raw1[0]))
+        damping(0, "rounded0")
+        first_stage(0, ["dealt3"])
         damping(1, "raw2")
         damping(2, "raw2")
         raw5.append(load_rows(w5[:, BANK:N], "raw2"))
-        first_stage(1, round_dealt(raw1[1]))
+        first_stage(1, ["dealt0"])
         duty_rows.append(load_rows(duty[:, BANK:S], "raw3"))
-        first_stage(2, round_dealt(raw1[2]))
+        first_stage(2, ["dealt1", "dealt2"])
         damping(3, "raw4")
 
-        w5q = []
-        for part, raw in enumerate(raw5):
-            rounded = staged(raw.shape[2])
-            nc.scalar.copy(out=woven(rounded), in_=by_fours(raw[:]))
-            w5q.append(rounded)
+        rounded5 = [round_plain(raw5[0], "square3"), round_plain(raw5[1], "square2")]
 
-        def weigh(h):
-            a32 = ring.tile([P, PACK, BANK], F32, name="quad", bufs=3, align_bytes=64)
+        def weigh(h, room):
+            a32 = place([P, PACK, BANK], F32, room)
             for t in range(PACK):
                 nc.vector.tensor_tensor(a32[:, t, :], acc1[h][t][:], duty_rows[h][:, t, :], MULT)
             return a32
 
-        def round_a(a32):
-            tile = staged(BANK)
-            nc.scalar.copy(out=woven(tile), in_=by_fours(a32[:]))
-            return tile
-
         def round_z(a32, h):
-            tile = staged(BANK)
+            tile = place([P, PACK * BANK], BF16, f"z{h}_rounded")
             nc.vector.tensor_tensor(woven(tile), by_fours(a32[:]), by_fours(damp[:, :, h * BANK : (h + 1) * BANK]), MULT)
             return tile
 
@@ -261,19 +255,18 @@ def tile_list_chain_wear_features_kernel(
                 out=yz[:], lhsT=w4[:, 2 * n * P : 2 * (n + 1) * P].bitcast(FP4X4), lhsT_scale=s4[:, n * P : (n + 1) * P],
                 rhs=zq[0][:].bitcast(FP8X4), rhs_scale=zq[1][:], start=True, stop=True,
             )
-            ya_sb = ring.tile([P, BANK], F32, name="evac", bufs=4)
+            ya_sb = place([P, BANK], F32, "ya", bufs=4)
             nc.scalar.copy(out=ya_sb[:], in_=ya[:])
-            result = ring.tile([P, BANK], F32, name="result", bufs=4)
+            result = place([P, BANK], F32, "result", bufs=4)
             nc.vector.tensor_tensor(result[:], yz[:], ya_sb[:], MAX)
             nc.sync.dma_start(out=out[n * P : (n + 1) * P, h * BANK : (h + 1) * BANK], in_=result[:])
 
-        a0 = weigh(0)
-        w5q[0] = quantise(w5q[0], "w5_0")
-        w5q[1] = quantise(w5q[1], "w5_1")
-        ra0 = round_a(a0)
+        a0 = weigh(0, "words2_1")
+        w5q = [quantise(rounded5[0], "w5_0"), quantise(rounded5[1], "w5_1")]
+        ra0 = round_plain(a0, "rounded0")
         rz0 = round_z(a0, 0)
-        a1 = weigh(1)
-        ra1 = round_a(a1)
+        a1 = weigh(1, "spread")
+        ra1 = round_plain(a1, "rounded1")
         zq0 = quantise(rz0, "z0")
         aq0 = quantise(ra0, "a0")
         rz1 = round_z(a1, 1)

@@ -48,12 +48,12 @@ def tile_list_chain_wear_features_kernel(
             nc.sync.dma_start(tile[:], src)
             return tile
 
-        def load_scale_rows(src, room, queue):
+        def load_scale_rows(src, room):
             passes, rows, width = src.shape
             tile = place([P, width], U8, room)
             nc.vector.memset(tile[:].bitcast(I32), 0)
             for q in range(QUADS):
-                queue.dma_start(
+                nc.sync.dma_start(
                     out=tile[32 * q : 32 * q + 4 * passes, :].bitcast(I32),
                     in_=src[:, 4 * q : 4 * q + 4, :].bitcast(I32),
                 )
@@ -114,31 +114,34 @@ def tile_list_chain_wear_features_kernel(
 
         ident = place([P, P], F32, "ident")
         make_identity(nc, ident[:])
-        s1 = load_scale_rows(tab_scales, "s1", nc.gpsimd)
-        s2 = load_scale_rows(tab2_scales, "s2", nc.gpsimd)
         wg = place([P, L], F32, "wg")
         nc.sync.dma_start(out=wg[:], in_=wgs)
         raw2 = [load_rows(w2[0:K_PASS, :], "raw0")]
         list2 = load_list(offs2, "list2")
-        list1 = load_list(offs, "list1")
-        places = load_list(pos1, "places")
         words2 = [load_words(tab2_words[0], "words2_0")]
         raw2.append(load_rows(w2[K_PASS : 2 * K_PASS, :], "raw1"))
-        words2.append(load_words(tab2_words[1], "words2_1"))
+        s2 = load_scale_rows(tab2_scales, "s2")
+
+        pages = []
+        for t in range(PACK):
+            page = place([P, S], F32, f"page{t}")
+            nc.vector.memset(page[:], 0.0)
+            pages.append(page)
 
         turned = bank(7)
         for b in range(L // P):
             nc.tensor.transpose(turned[:, b * P : (b + 1) * P], wg[:, b * P : (b + 1) * P], ident[:])
+        words2.append(load_words(tab2_words[1], "wg"))
+        list1 = load_list(offs, "list1")
+        places = load_list(pos1, "places")
         spread = place([P, L // P, PACK, QUADS, 32], F32, "spread")
         for q in range(QUADS):
             nc.scalar.copy(out=spread[:, :, :, q, :], in_=turned[:].rearrange("p (b m t) -> p b t m", b=L // P, t=PACK))
 
-        gs1 = gather(s1, list1[:], S, U8, "gs1")
-        gs2 = gather(s2, list2[:], L, U8, "gs2")
-
         rounded = round_dealt(raw2[0], "rounded0")
         g2 = [gather(words2[0], list2[:], L, U32, "g2_0")]
         w2q = [quantise(rounded, "w2_0")]
+        gs2 = gather(s2, list2[:], L, U8, "gs2")
 
         dealt, backs = [], []
         for t in range(PACK):
@@ -158,32 +161,24 @@ def tile_list_chain_wear_features_kernel(
         deal(1)
 
         w2q.append(quantise(round_dealt(raw2[1], "rounded1"), "w2_1"))
-        g2.append(gather(words2[1], list2[:], L, U32, "s1"))
-
-        pages = []
-        for room in ("wg", "spread", "words2_0", "s2"):
-            page = place([P, S], F32, room)
-            nc.gpsimd.memset(page[:], 0.0)
-            pages.append(page)
+        g2.append(gather(words2[1], list2[:], L, U32, "g2_1"))
 
         acc2 = [bank(4 + t) for t in range(PACK)]
         for a in range(passes2):
             for t in range(PACK):
                 first_stage_pass(acc2[t], w2q[a], t, g2[a][:], gs2[4 * a : P, :], a, passes2)
 
-        words1, raw1 = [], []
-        for a in range(passes1):
-            if a < passes1 - 1:
-                words1.append(load_words(tab_words[a], f"words1_{a}"))
-                raw1.append(load_rows(w1[a * K_PASS : (a + 1) * K_PASS, :], f"raw{2 + a}"))
-            else:
-                raw1.append(load_rows(w1[a * K_PASS : (a + 1) * K_PASS, :], f"raw{2 + a}"))
-                words1.append(load_words(tab_words[a], f"words1_{a}"))
-        duty_rows = [load_rows(duty[:, 0:BANK], "raw0")]
-        s4 = load_scale_rows(w4_scales, "s4", nc.sync)
-        w4 = place([P, 2 * N], U8, "w4")
+        def w1_rows(a):
+            return w1[a * K_PASS : (a + 1) * K_PASS, :]
+
+        words1 = [load_words(tab_words[0], "words2_0")]
+        raw1 = [load_rows(w1_rows(0), "raw0"), load_rows(w1_rows(1), "spread")]
+        s1 = load_scale_rows(tab_scales, "rounded0")
+        raw1.append(load_rows(w1_rows(2), "raw1"))
+        words1.append(load_words(tab_words[1], "wg"))
+        s4 = load_scale_rows(w4_scales, "gs2")
+        w4 = place([P, 2 * N], U8, "g2_0")
         nc.sync.dma_start(out=w4[:].bitcast(I32), in_=w4_words[0].bitcast(I32))
-        raw5 = [load_rows(w5[:, 0:BANK], "raw1")]
 
         damp = place([P, PACK, S], F32, "damp")
         squares = []
@@ -195,6 +190,9 @@ def tile_list_chain_wear_features_kernel(
         deal(3)
         for t in range(PACK):
             nc.vector.tensor_tensor(pages[t][:].indirect(places[:]), squares[t][:], dealt[t][:], MULT)
+        words1.append(load_words(tab_words[2], "square0"))
+        duty_rows = [load_rows(duty[:, 0:BANK], "square1")]
+        gs1 = gather(s1, list1[:], S, U8, "square3")
 
         def damping(t, room):
             root = place([P, S], F32, room)
@@ -219,17 +217,17 @@ def tile_list_chain_wear_features_kernel(
                 for t in range(PACK):
                     first_stage_pass(acc1[h][t], wq, t, picked[h], gs1[4 * a : P, h * BANK : (h + 1) * BANK], a, passes1)
 
-        damping(0, "rounded0")
+        damping(0, "root0")
         first_stage(0, ["dealt3"])
-        damping(1, "raw2")
-        damping(2, "raw2")
-        raw5.append(load_rows(w5[:, BANK:N], "raw2"))
+        damping(1, "raw0")
+        damping(2, "raw0")
         first_stage(1, ["dealt0"])
-        duty_rows.append(load_rows(duty[:, BANK:S], "raw3"))
+        raw5 = [load_rows(w5[:, 0:BANK], "raw0"), load_rows(w5[:, BANK:N], "spread")]
         first_stage(2, ["dealt1", "dealt2"])
-        damping(3, "raw4")
+        damping(3, "raw1")
+        duty_rows.append(load_rows(duty[:, BANK:S], "raw1"))
 
-        rounded5 = [round_plain(raw5[0], "square3"), round_plain(raw5[1], "square2")]
+        rounded5 = [round_plain(raw5[0], "w5_0_rounded"), round_plain(raw5[1], "w5_1_rounded")]
 
         def weigh(h, room):
             a32 = place([P, PACK, BANK], F32, room)
@@ -261,11 +259,11 @@ def tile_list_chain_wear_features_kernel(
             nc.vector.tensor_tensor(result[:], yz[:], ya_sb[:], MAX)
             nc.sync.dma_start(out=out[n * P : (n + 1) * P, h * BANK : (h + 1) * BANK], in_=result[:])
 
-        a0 = weigh(0, "words2_1")
+        a0 = weigh(0, "wg")
         w5q = [quantise(rounded5[0], "w5_0"), quantise(rounded5[1], "w5_1")]
         ra0 = round_plain(a0, "rounded0")
         rz0 = round_z(a0, 0)
-        a1 = weigh(1, "spread")
+        a1 = weigh(1, "words2_0")
         ra1 = round_plain(a1, "rounded1")
         zq0 = quantise(rz0, "z0")
         aq0 = quantise(ra0, "a0")

@@ -201,33 +201,26 @@ def tile_list_chain_wear_features_kernel(
 
         acc1 = [[bank(PACK * h + t) for t in range(PACK)] for h in range(HALVES)]
 
-        def first_stage(a, rooms):
-            rounded = round_dealt(raw1[a], f"dealt{a}")
-            if len(rooms) == 1:
-                whole = gather(words1[a], list1[:], S, U32, rooms[0])
-                picked = [whole[:, h * BANK : (h + 1) * BANK] for h in range(HALVES)]
-                wq = quantise(rounded, f"w1_{a}")
-            else:
-                wq = quantise(rounded, f"w1_{a}")
-                picked = [
-                    gather(words1[a], list1[:, h * BANK // 16 : (h + 1) * BANK // 16], BANK, U32, rooms[h])[:]
-                    for h in range(HALVES)
-                ]
+        def first_stage(a):
+            wq = quantise(round_dealt(raw1[a], f"dealt{a}"), f"w1_{a}")
+            picked = place([P, S], U32, f"dealt{a}")
             for h in range(HALVES):
+                cols = slice(h * BANK, (h + 1) * BANK)
+                offsets = list1[:, h * BANK // 16 : (h + 1) * BANK // 16]
+                nc.vector.tensor_copy(picked[:, cols], words1[a][:].indirect(offsets))
                 for t in range(PACK):
-                    first_stage_pass(acc1[h][t], wq, t, picked[h], gs1[4 * a : P, h * BANK : (h + 1) * BANK], a, passes1)
+                    first_stage_pass(acc1[h][t], wq, t, picked[:, cols], gs1[4 * a : P, cols], a, passes1)
 
         damping(0, "root0")
-        first_stage(0, ["dealt3"])
-        damping(1, "raw0")
-        damping(2, "raw0")
-        first_stage(1, ["dealt0"])
-        raw5 = [load_rows(w5[:, 0:BANK], "raw0"), load_rows(w5[:, BANK:N], "spread")]
-        first_stage(2, ["dealt1", "dealt2"])
+        first_stage(0)
+        raw5 = [load_rows(w5[:, 0:BANK], "raw0")]
+        first_stage(1)
+        damping(1, "spread")
+        duty_rows.append(load_rows(duty[:, BANK:S], "spread"))
+        first_stage(2)
+        damping(2, "raw1")
         damping(3, "raw1")
-        duty_rows.append(load_rows(duty[:, BANK:S], "raw1"))
-
-        rounded5 = [round_plain(raw5[0], "w5_0_rounded"), round_plain(raw5[1], "w5_1_rounded")]
+        raw5.append(load_rows(w5[:, BANK:N], "raw1"))
 
         def weigh(h, room):
             a32 = place([P, PACK, BANK], F32, room)
@@ -259,15 +252,18 @@ def tile_list_chain_wear_features_kernel(
             nc.vector.tensor_tensor(result[:], yz[:], ya_sb[:], MAX)
             nc.sync.dma_start(out=out[n * P : (n + 1) * P, h * BANK : (h + 1) * BANK], in_=result[:])
 
+        rounded5 = round_plain(raw5[0], "w5_0_rounded")
         a0 = weigh(0, "wg")
-        w5q = [quantise(rounded5[0], "w5_0"), quantise(rounded5[1], "w5_1")]
         ra0 = round_plain(a0, "rounded0")
         rz0 = round_z(a0, 0)
         a1 = weigh(1, "words2_0")
+        w5q = [quantise(rounded5, "w5_0")]
+        rounded5 = round_plain(raw5[1], "w5_1_rounded")
         ra1 = round_plain(a1, "rounded1")
-        zq0 = quantise(rz0, "z0")
         aq0 = quantise(ra0, "a0")
+        zq0 = quantise(rz0, "z0")
         rz1 = round_z(a1, 1)
+        w5q.append(quantise(rounded5, "w5_1"))
         for n in range(3):
             second_stage(0, n, aq0, zq0)
         zq1 = quantise(rz1, "z1")

from contextlib import ExitStack

import concourse.mybir as mybir
from concourse.masks import make_identity

T, S, T3, L, K, K2, H, N = 4096, 1024, 2048, 512, 1536, 1024, 512, 768
FLOPS = 2 * (K * H * S + K2 * H * L + 2 * H * N * S)

F32 = mybir.dt.float32
BF16 = mybir.dt.bfloat16
I32 = mybir.dt.int32
U32 = mybir.dt.uint32
U16 = mybir.dt.uint16
U8 = mybir.dt.uint8
FP8X4 = mybir.dt.float8_e4m3fn_x4
FP4X4 = mybir.dt.float4_e2m1fn_x4
MULT = mybir.AluOpType.mult
MAX = mybir.AluOpType.max
ACT = mybir.ActivationFunctionType

P = 128
PACK = 4
K_PASS = P * PACK
BANK = 512
QUADS = 4
HALVES = S // BANK


def tile_list_chain_wear_features_kernel(
    tc, tab_words, tab_scales, offs, tab2_words, tab2_scales, offs2, pos1, w1, w2, duty, wgs, w4_words, w4_scales, w5, out
):
    nc = tc.nc
    passes1 = K // K_PASS
    passes2 = K2 // K_PASS

    with ExitStack() as ctx:
        sbuf = ctx.enter_context(tc.tile_pool(name="sbuf", bufs=1))
        psum = ctx.enter_context(tc.psum_pool(name="psum", bufs=1))

        def place(shape, dtype, room, bufs=1):
            return sbuf.tile(shape, dtype, name=room, bufs=bufs, align_bytes=64)

        def bank(i):
            return psum.tile([P, BANK], F32, name=f"bank{i}")

        def load_list(src, room):
            tile = place(list(src.shape), U16, room)
            nc.sync.dma_start(tile[:], src)
            return tile

        def load_scale_rows(src, room):
            passes, rows, width = src.shape
            tile = place([P, width], U8, room)
            nc.vector.memset(tile[:].bitcast(I32), 0)
            for q in range(QUADS):
                nc.sync.dma_start(
                    out=tile[32 * q : 32 * q + 4 * passes, :].bitcast(I32),
                    in_=src[:, 4 * q : 4 * q + 4, :].bitcast(I32),
                )
            return tile

        def load_words(src, room):
            tile = place([P, src.shape[1]], U32, room)
            nc.sync.dma_start(out=tile[:].bitcast(I32), in_=src.rearrange("p t i -> p (t i)").bitcast(I32))
            return tile

        def load_rows(src, room):
            tile = place([P, PACK, src.shape[1]], F32, room)
            nc.sync.dma_start(out=tile[:], in_=src.rearrange("(p j) w -> p j w", j=PACK))
            return tile

        def gather(window, offsets, count, dtype, room):
            tile = place([P, count], dtype, room)
            nc.vector.tensor_copy(tile[:], window[:].indirect(offsets))
            return tile

        def round_dealt(raw, room):
            tile = place([P, PACK * H], BF16, room)
            nc.scalar.copy(
                out=tile[:].rearrange("p (t m j) -> p m j t", t=PACK, j=PACK),
                in_=raw[:].rearrange("p j (m t) -> p m j t", t=PACK),
            )
            return tile

        def woven(tile):
            return tile[:].rearrange("p (c i j) -> p c j i", i=4, j=PACK)

        def by_fours(rows):
            return rows.rearrange("p j (c i) -> p c j i", i=4)

        def round_plain(rows, room):
            tile = place([P, PACK * rows.shape[2]], BF16, room)
            nc.scalar.copy(out=woven(tile), in_=by_fours(rows[:]))
            return tile

        def quantise(rounded, name):
            width = rounded.shape[1] // PACK
            codes = place([P, width], U32, name + "_codes")
            scales = place([P, width], U8, name + "_scales")
            nc.vector.quantize_mx(out=codes[:].bitcast(FP8X4), scales=scales[:], in_=rounded[:])
            return codes, scales

        def first_stage_pass(acc, weight, t, words, scale_rows, a, passes):
            cols = slice(t * P, (t + 1) * P)
            nc.tensor.matmul_mx(
                out=acc[:],
                lhsT=weight[0][:, cols].bitcast(FP8X4),
                lhsT_scale=weight[1][:, cols],
                rhs=words.bitcast(FP8X4),
                rhs_scale=scale_rows,
                start=(a == 0),
                stop=(a == passes - 1),
            )

        ident = place([P, P], F32, "ident")
        make_identity(nc, ident[:])
        wg = place([P, L], F32, "wg")
        nc.sync.dma_start(out=wg[:], in_=wgs)
        raw2 = [load_rows(w2[0:K_PASS, :], "raw0")]
        list2 = load_list(offs2, "list2")
        words2 = [load_words(tab2_words[0], "words2_0")]
        raw2.append(load_rows(w2[K_PASS : 2 * K_PASS, :], "raw1"))
        s2 = load_scale_rows(tab2_scales, "s2")

        pages = []
        for t in range(PACK):
            page = place([P, S], F32, f"page{t}")
            nc.vector.memset(page[:], 0.0)
            pages.append(page)

        turned = bank(7)
        for b in range(L // P):
            nc.tensor.transpose(turned[:, b * P : (b + 1) * P], wg[:, b * P : (b + 1) * P], ident[:])
        words2.append(load_words(tab2_words[1], "wg"))
        list1 = load_list(offs, "list1")
        places = load_list(pos1, "places")
        spread = place([P, L // P, PACK, QUADS, 32], F32, "spread")
        for q in range(QUADS):
            nc.scalar.copy(out=spread[:, :, :, q, :], in_=turned[:].rearrange("p (b m t) -> p b t m", b=L // P, t=PACK))

        rounded = round_dealt(raw2[0], "rounded0")
        g2 = [gather(words2[0], list2[:], L, U32, "g2_0")]
        w2q = [quantise(rounded, "w2_0")]
        gs2 = gather(s2, list2[:], L, U8, "gs2")

        dealt, backs = [], []
        for t in range(PACK):
            back = bank(t)
            for b in range(L // P):
                nc.tensor.transpose(
                    back[:, b * P : (b + 1) * P], spread[:, b, t, :, :].rearrange("p q m -> p (q m)"), ident[:]
                )
            backs.append(back)

        def deal(t):
            tile = place([P, L], F32, f"dealt{t}")
            nc.scalar.copy(out=tile[:], in_=backs[t][:])
            dealt.append(tile)

        deal(0)
        deal(1)

        w2q.append(quantise(round_dealt(raw2[1], "rounded1"), "w2_1"))
        g2.append(gather(words2[1], list2[:], L, U32, "g2_1"))

        acc2 = [bank(4 + t) for t in range(PACK)]
        for a in range(passes2):
            for t in range(PACK):
                first_stage_pass(acc2[t], w2q[a], t, g2[a][:], gs2[4 * a : P, :], a, passes2)

        def w1_rows(a):
            return w1[a * K_PASS : (a + 1) * K_PASS, :]

        words1 = [load_words(tab_words[0], "words2_0")]
        raw1 = [load_rows(w1_rows(0), "raw0"), load_rows(w1_rows(1), "spread")]
        s1 = load_scale_rows(tab_scales, "rounded0")
        raw1.append(load_rows(w1_rows(2), "raw1"))
        words1.append(load_words(tab_words[1], "wg"))
        s4 = load_scale_rows(w4_scales, "gs2")
        w4 = place([P, 2 * N], U8, "g2_0")
        nc.sync.dma_start(out=w4[:].bitcast(I32), in_=w4_words[0].bitcast(I32))

        damp = place([P, PACK, S], F32, "damp")
        squares = []
        for t in range(PACK):
            sq = place([P, L], F32, f"square{t}")
            nc.scalar.activation(out=sq[:], in_=acc2[t][:], func=ACT.Square)
            squares.append(sq)
        deal(2)
        deal(3)
        for t in range(PACK):
            nc.vector.tensor_tensor(pages[t][:].indirect(places[:]), squares[t][:], dealt[t][:], MULT)
        words1.append(load_words(tab_words[2], "square0"))
        duty_rows = [load_rows(duty[:, 0:BANK], "square1")]
        gs1 = gather(s1, list1[:], S, U8, "square3")

        def damping(t, room):
            root = place([P, S], F32, room)
            nc.scalar.activation(out=root[:], in_=pages[t][:], func=ACT.Abs_reciprocal_sqrt, bias=1.0)
            nc.scalar.activation(out=damp[:, t, :], in_=root[:], func=ACT.Square)

        acc1 = [[bank(PACK * h + t) for t in range(PACK)] for h in range(HALVES)]

        def first_stage(a):
            wq = quantise(round_dealt(raw1[a], f"dealt{a}"), f"w1_{a}")
            picked = place([P, S], U32, f"dealt{a}")
            for h in range(HALVES):
                cols = slice(h * BANK, (h + 1) * BANK)
                offsets = list1[:, h * BANK // 16 : (h + 1) * BANK // 16]
                nc.vector.tensor_copy(picked[:, cols], words1[a][:].indirect(offsets))
                for t in range(PACK):
                    first_stage_pass(acc1[h][t], wq, t, picked[:, cols], gs1[4 * a : P, cols], a, passes1)

        damping(0, "root0")
        first_stage(0)
        raw5 = [load_rows(w5[:, 0:BANK], "raw0")]
        first_stage(1)
        damping(1, "spread")
        duty_rows.append(load_rows(duty[:, BANK:S], "spread"))
        first_stage(2)
        damping(2, "raw1")
        damping(3, "raw1")
        raw5.append(load_rows(w5[:, BANK:N], "raw1"))

        def weigh(h, room):
            a32 = place([P, PACK, BANK], F32, room)
            for t in range(PACK):
                nc.vector.tensor_tensor(a32[:, t, :], acc1[h][t][:], duty_rows[h][:, t, :], MULT)
            return a32

        def round_z(a32, h):
            tile = place([P, PACK * BANK], BF16, f"z{h}_rounded")
            nc.vector.tensor_tensor(woven(tile), by_fours(a32[:]), by_fours(damp[:, :, h * BANK : (h + 1) * BANK]), MULT)
            return tile

        def second_stage(h, n, aq, zq):
            pair = (h * (N // P) + n) % PACK
            part, first = divmod(n * P, BANK)
            cols = slice(first, first + P)
            ya, yz = bank(2 * pair), bank(2 * pair + 1)
            nc.tensor.matmul_mx(
                out=ya[:], lhsT=w5q[part][0][:, cols].bitcast(FP8X4), lhsT_scale=w5q[part][1][:, cols],
                rhs=aq[0][:].bitcast(FP8X4), rhs_scale=aq[1][:], start=True, stop=True,
            )
            nc.tensor.matmul_mx(
                out=yz[:], lhsT=w4[:, 2 * n * P : 2 * (n + 1) * P].bitcast(FP4X4), lhsT_scale=s4[:, n * P : (n + 1) * P],
                rhs=zq[0][:].bitcast(FP8X4), rhs_scale=zq[1][:], start=True, stop=True,
            )
            ya_sb = place([P, BANK], F32, "ya", bufs=4)
            nc.scalar.copy(out=ya_sb[:], in_=ya[:])
            result = place([P, BANK], F32, "result", bufs=4)
            nc.vector.tensor_tensor(result[:], yz[:], ya_sb[:], MAX)
            nc.sync.dma_start(out=out[n * P : (n + 1) * P, h * BANK : (h + 1) * BANK], in_=result[:])

        rounded5 = round_plain(raw5[0], "w5_0_rounded")
        a0 = weigh(0, "wg")
        ra0 = round_plain(a0, "rounded0")
        rz0 = round_z(a0, 0)
        a1 = weigh(1, "words2_0")
        w5q = [quantise(rounded5, "w5_0")]
        rounded5 = round_plain(raw5[1], "w5_1_rounded")
        ra1 = round_plain(a1, "rounded1")
        aq0 = quantise(ra0, "a0")
        zq0 = quantise(rz0, "z0")
        rz1 = round_z(a1, 1)
        w5q.append(quantise(rounded5, "w5_1"))
        for n in range(3):
            second_stage(0, n, aq0, zq0)
        zq1 = quantise(rz1, "z1")
        aq1 = quantise(ra1, "a1")
        for n in range(3, N // P):
            second_stage(0, n, aq0, zq0)
        for n in range(N // P):
            second_stage(1, n, aq1, zq1)
